import numpy as np
import ml_dtypes


def mxq(x, axis, fmt="e4m3"):
    dtype, down = {"e4m3": (ml_dtypes.float8_e4m3fn, 7), "e5m2": (ml_dtypes.float8_e5m2, 14)}[fmt]
    v = np.moveaxis(np.asarray(x, np.float32).astype(ml_dtypes.bfloat16).astype(np.float64), axis, -1)
    blocks = v.reshape(v.shape[:-1] + (-1, 32))
    amax = np.abs(blocks).max(-1, keepdims=True)
    byte = np.maximum(np.where(amax > 0, np.frexp(amax)[1] - 1 + 127, 0) - down, 1)
    scale = np.exp2(byte - 127.0)
    codes = (blocks / scale).astype(np.float32).astype(dtype).astype(np.float64)
    return np.moveaxis((codes * scale).reshape(v.shape), -1, axis)


WIDE = False


def mx_kscale(k):
    if not WIDE:
        return np.ones(k)
    levels = np.array([24, -24, 12, -12, 0])
    if k % 512:
        return np.exp2(np.random.permutation(np.resize(levels, k // 32))).repeat(32)
    a = np.empty((k // 512, 16))
    for p in range(k // 512):
        a[p, :8] = np.random.permutation(np.resize(levels, 8))
        for g in range(8):
            far = levels[np.abs(levels - a[p, g]) >= 10]
            a[p, g + 8] = far[np.random.randint(len(far))]
    return np.exp2(a.ravel()).repeat(32)


def f64(x):
    return np.asarray(x).astype(np.float64)


def striped(idx):
    return np.tile(idx.reshape(-1, 16).T, (8, 1)).astype(np.uint16)


def unstriped(offs):
    return offs[:16].T.reshape(-1).astype(np.int64)


E2M1 = np.array([0.0, 0.5, 1.0, 1.5, 2.0, 3.0, 4.0, 6.0, -0.0, -0.5, -1.0, -1.5, -2.0, -3.0, -4.0, -6.0])


def pack_weight(w, fmt):
    k, n = w.shape
    w = f64(np.asarray(w, np.float32).astype(ml_dtypes.bfloat16)).reshape(k // 32, 32, n)
    amax = np.abs(w).max(1)
    if fmt == "e4m3":
        byte = np.frexp(amax)[1] - 1 + 127 - 7
    else:
        mant, ex = np.frexp(amax / 6.0)
        byte = np.where(mant > 0.5, ex, ex - 1) + 127
    byte = np.clip(np.where(amax > 0, byte, 1), 1, 254)
    scaled = (w * np.exp2(127.0 - byte)[:, None, :]).reshape(k, n).astype(np.float32)
    by_word = np.ascontiguousarray(scaled.reshape(k // 512, 128, 4, n).transpose(0, 1, 3, 2))
    if fmt == "e4m3":
        words = by_word.astype(ml_dtypes.float8_e4m3fn).view(np.uint8)
    else:
        c = by_word.astype(ml_dtypes.float4_e2m1fn).view(np.uint8) & 0xF
        words = (c[..., 0::2] | (c[..., 1::2] << 4)).reshape(k // 512, 128, 2 * n)
    return np.ascontiguousarray(words), np.ascontiguousarray(byte.astype(np.uint8).reshape(k // 512, 16, n))


def unpack_weight(words, scales, fmt):
    g, _, n = scales.shape
    words = np.ascontiguousarray(words).reshape(g, 128, n, -1)
    if fmt == "e4m3":
        vals = words.view(ml_dtypes.float8_e4m3fn).astype(np.float64)
    else:
        nib = np.empty((g, 128, n, 4), np.uint8)
        nib[..., 0::2] = words & 0xF
        nib[..., 1::2] = words >> 4
        vals = E2M1[nib]
    vals = vals * np.repeat(np.exp2(scales.astype(np.float64) - 127.0), 8, axis=1)[..., None]
    return vals.transpose(0, 1, 3, 2).reshape(g * 512, n)


def planes(y):
    n, m = y.shape
    v = y.astype(np.float32).astype(ml_dtypes.bfloat16).astype(np.float64).reshape(n // 32, 32, m)
    top = np.abs(v).max(1)
    byte = np.clip(np.where(top > 0, np.frexp(top)[1] - 1 + 127 - 7, 1), 1, 254)
    codes = (v * np.exp2(127.0 - byte)[:, None, :]).reshape(n, m).astype(np.float32).astype(ml_dtypes.float8_e4m3fn).view(np.uint8)
    words = codes.reshape(n // 512, 128, 4, m).transpose(0, 1, 3, 2)
    return np.ascontiguousarray(words), np.ascontiguousarray(byte.astype(np.uint8).reshape(n // 512, 16, m))


K, R, N, T, J = 512, 512, 512, 2048, 1024


def setup_inputs():
    n = np.random.standard_normal
    s = mx_kscale(K)[:, None]
    u = mx_kscale(R)[:, None]
    p_tab = pack_weight(n((K, T)) * s, "e4m3")
    p_wu = pack_weight(n((K, R)) / np.sqrt(K) / s * u.T, "e2m1")
    return {
        "tab_words": p_tab[0],
        "tab_scales": p_tab[1],
        "wg": (n((K, R)) / np.sqrt(K) / s).astype(np.float32),
        "wu_words": p_wu[0],
        "wu_scales": p_wu[1],
        "wd": (n((R, N)) / np.sqrt(R) / u).astype(np.float32),
        "rT": (n((N, T))).astype(np.float32),
        "offs": striped(np.random.permutation(T)[:J]),
    }


def reference(tab_words, tab_scales, wg, wu_words, wu_scales, wd, rT, offs):
    idx = unstriped(offs)
    tab_ = unpack_weight(tab_words, tab_scales, "e4m3")[:, idx]
    wg_ = mxq(f64(wg), 0, "e4m3")
    wu_ = unpack_weight(wu_words, wu_scales, "e2m1")
    ga = wg_.T @ tab_
    ub = wu_.T @ tab_
    h = np.maximum(ga, 0.0) * ub
    h_ = mxq(h, 0, "e4m3")
    wd_ = mxq(f64(wd), 0, "e4m3")
    y = wd_.T @ h_
    out_0 = y + f64(rT)[:, idx]
    return (out_0,) + planes(out_0)

@@ -1,0 +1,192 @@
+from contextlib import ExitStack
+
+import concourse.mybir as mybir
+
+K, R, N, T, J = 512, 512, 512, 2048, 1024
+FLOPS = 2 * J * (K * R + K * R + R * N)
+
+F32 = mybir.dt.float32
+BF16 = mybir.dt.bfloat16
+I32 = mybir.dt.int32
+U32 = mybir.dt.uint32
+U16 = mybir.dt.uint16
+U8 = mybir.dt.uint8
+FP8X4 = mybir.dt.float8_e4m3fn_x4
+FP4X4 = mybir.dt.float4_e2m1fn_x4
+ALU = mybir.AluOpType
+
+P = 128
+PACK = 4
+STEP = 128
+CHUNK = 256
+WORD_PIECES = (256, 256, 512)
+OUT_PIECES = (256, 256, 256, 128, 128)
+
+
+def starts(widths):
+    return [(sum(widths[:i]), w) for i, w in enumerate(widths)]
+
+
+def tile_list_gmlpt_relu_resLP_kernel(
+    tc, tab_words, tab_scales, wg, wu_words, wu_scales, wd, rT, offs, out_0, out_1, out_2
+):
+    nc = tc.nc
+    with ExitStack() as ctx:
+        keep = ctx.enter_context(tc.tile_pool(name="keep", bufs=1))
+        ring = ctx.enter_context(tc.tile_pool(name="ring", bufs=2))
+        psum = ctx.enter_context(tc.psum_pool(name="psum", bufs=2))
+
+        offsets = keep.tile([P, J // 16], U16, name="offsets")
+        tab_s = keep.tile([P, T], U8, name="tab_s", align_bytes=64)
+        wu_s_raw = keep.tile([P, R], U8, name="wu_s_raw", align_bytes=64)
+        tab_w = keep.tile([P, T], I32, name="tab_w", align_bytes=64)
+        wu_w_raw = keep.tile([P, R // 2], I32, name="wu_w_raw", align_bytes=64)
+        wg_raw = [keep.tile([P, PACK, R // 2], F32, name="wg_raw%d" % u) for u in range(2)]
+        wd_raw = keep.tile([P, PACK, N], F32, name="wd_raw")
+        r_tab = [keep.tile([P, T], F32, name="r_tab%d" % t) for t in range(PACK)]
+
+        nc.vector.memset(tab_s[:].bitcast(I32), 0)
+        nc.vector.memset(wu_s_raw[:].bitcast(I32), 0)
+
+        def load_scale_rows(plane, rows):
+            for q in range(4):
+                nc.sync.dma_start(out=plane[32 * q : 32 * q + 4, :].bitcast(I32), in_=rows[0, 4 * q : 4 * q + 4, :].bitcast(I32))
+
+        def load_tab_w():
+            nc.sync.dma_start(out=tab_w[:], in_=tab_words[0].rearrange("p t i -> p (t i)").bitcast(I32))
+
+        def load_wg(u):
+            nc.sync.dma_start(out=wg_raw[u][:], in_=wg.rearrange("(p j) r -> p j r", j=PACK)[:, :, u * (R // 2) : (u + 1) * (R // 2)])
+
+        nc.sync.dma_start(offsets[:], offs)
+        load_scale_rows(tab_s, tab_scales)
+        nc.sync.dma_start(out=wu_w_raw[:], in_=wu_words[0].bitcast(I32))
+        load_wg(0)
+        load_wg(1)
+        load_tab_w()
+        load_scale_rows(wu_s_raw, wu_scales)
+        r_rows = rT.rearrange("(p t) c -> t p c", t=PACK)
+        nc.sync.dma_start(out=wd_raw[:], in_=wd.rearrange("(p j) n -> p j n", j=PACK))
+        for t in range(PACK):
+            nc.sync.dma_start(out=r_tab[t][:], in_=r_rows[t])
+
+        def picks(j0, width):
+            return offsets[:, j0 // 16 : (j0 + width) // 16]
+
+        v_s = keep.tile([P, J], U8, name="v_s", align_bytes=64)
+        nc.vector.tensor_copy(out=v_s[:], in_=tab_s[:].indirect(offsets[:]))
+
+        wu_w = keep.tile([P, PACK, P], U16, name="wu_w", align_bytes=64)
+        wu_s = keep.tile([P, PACK, P], U8, name="wu_s", align_bytes=64)
+        nc.scalar.copy(out=wu_w[:], in_=wu_w_raw[:].bitcast(U16).rearrange("p (m t) -> p t m", t=PACK))
+        nc.vector.tensor_copy(out=wu_s[:], in_=wu_s_raw[:].rearrange("p (m t) -> p t m", t=PACK))
+
+        def round_and_deal(dst, src, m0, count, eng):
+            eng(
+                out=dst[:, :, m0 : m0 + count, :].rearrange("p t m j -> p m t j"),
+                in_=src.rearrange("p j (m t) -> p m t j", t=PACK),
+            )
+
+        wg_b = keep.tile([P, PACK, P, PACK], BF16, name="wg_b", align_bytes=64)
+        round_and_deal(wg_b, wg_raw[0][:], 0, P // 2, nc.scalar.copy)
+        round_and_deal(wg_b, wg_raw[1][:], P // 2, P // 2, nc.scalar.copy)
+        wg_w = keep.tile([P, R], U32, name="wg_w", align_bytes=64)
+        wg_s = keep.tile([P, R], U8, name="wg_s", align_bytes=64)
+        nc.vector.quantize_mx(out=wg_w[:].bitcast(FP8X4), scales=wg_s[:], in_=wg_b[:].rearrange("p t m j -> p (t m j)"))
+
+        v_w = keep.tile([P, J], U32, name="v_w", align_bytes=64)
+
+        def gather_words(j0, width):
+            nc.vector.tensor_copy(out=v_w[:, j0 : j0 + width], in_=tab_w[:].bitcast(U32).indirect(picks(j0, width)))
+
+        wd_b = keep.tile([P, PACK, P, PACK], BF16, name="wd_b", align_bytes=64)
+        wd_w = keep.tile([P, N], U32, name="wd_w", align_bytes=64)
+        wd_s = keep.tile([P, N], U8, name="wd_s", align_bytes=64)
+
+        h_w = keep.tile([P, J], U32, name="h_w", align_bytes=64)
+        h_s = keep.tile([P, J], U8, name="h_s", align_bytes=64)
+        h_b = keep.tile([P, J * PACK], BF16, name="h_b", align_bytes=64)
+
+        def hidden(j0):
+            cols = slice(j0, j0 + STEP)
+            moving = v_w[:, cols].bitcast(FP8X4)
+            ub = psum.tile([P, PACK, STEP], F32, name="ub")
+            ga = psum.tile([P, PACK, STEP], F32, name="ga")
+            for t in range(PACK):
+                nc.tensor.matmul_mx(out=ub[:, t, :], lhsT=wu_w[:, t, :].bitcast(FP4X4), lhsT_scale=wu_s[:, t, :], rhs=moving, rhs_scale=v_s[:, cols], start=True, stop=True)
+            for t in range(PACK):
+                m = slice(t * P, (t + 1) * P)
+                nc.tensor.matmul_mx(out=ga[:, t, :], lhsT=wg_w[:, m].bitcast(FP8X4), lhsT_scale=wg_s[:, m], rhs=moving, rhs_scale=v_s[:, cols], start=True, stop=True)
+            ub_sb = ring.tile([P, STEP, PACK], F32, name="ub_sb", bufs=4)
+            nc.scalar.copy(out=ub_sb[:], in_=ub[:].rearrange("p t n -> p n t"))
+            nc.vector.scalar_tensor_tensor(
+                out=h_b[:, j0 * PACK : (j0 + STEP) * PACK].rearrange("p (n t) -> p n t", t=PACK),
+                in0=ga[:].rearrange("p t n -> p n t"), scalar=0.0, in1=ub_sb[:], op0=ALU.max, op1=ALU.mult,
+            )
+
+        def quantize_h(j0):
+            cols = slice(j0, j0 + CHUNK)
+            nc.vector.quantize_mx(out=h_w[:, cols].bitcast(FP8X4), scales=h_s[:, cols], in_=h_b[:, j0 * PACK : (j0 + CHUNK) * PACK])
+
+        word_pieces = dict(starts(WORD_PIECES))
+        gather_words(0, word_pieces[0])
+        for s in range(J // STEP):
+            j0 = s * STEP
+            if j0 + STEP in word_pieces:
+                gather_words(j0 + STEP, word_pieces[j0 + STEP])
+            hidden(j0)
+            if j0 % CHUNK == 0 and j0 > 0:
+                quantize_h(j0 - CHUNK)
+            if 1 <= s < 1 + 4:
+                i = s - 1
+                round_and_deal(wd_b, wd_raw[:, :, i * P : (i + 1) * P], i * (P // 4), P // 4, nc.scalar.copy)
+            if s == 1 + 4:
+                nc.vector.quantize_mx(out=wd_w[:].bitcast(FP8X4), scales=wd_s[:], in_=wd_b[:].rearrange("p t m j -> p (t m j)"))
+        quantize_h(J - CHUNK)
+
+        pieces = starts(OUT_PIECES)
+        res = [keep.tile([P, PACK, w], F32, name="res%d" % j0) for j0, w in pieces]
+        out_rows = out_0.rearrange("(p t) j -> p t j", t=PACK)
+        o_s = keep.tile([P, J], U8, name="o_s", align_bytes=64)
+        words_out = out_1[0].rearrange("p j i -> p (j i)").bitcast(I32)
+
+        def pair(c, e):
+            j0, width = pieces[c]
+            cols = slice(j0, j0 + width)
+            y = psum.tile([P, 2, width], F32, name="y%d" % e)
+            for i in range(2):
+                m = slice((2 * e + i) * P, (2 * e + i + 1) * P)
+                nc.tensor.matmul_mx(
+                    out=y[:, i, :], lhsT=wd_w[:, m].bitcast(FP8X4), lhsT_scale=wd_s[:, m],
+                    rhs=h_w[:, cols].bitcast(FP8X4), rhs_scale=h_s[:, cols], start=True, stop=True,
+                )
+            y_sb = ring.tile([P, 2, width], F32, name="y_sb%d" % e, bufs=len(pieces))
+            nc.scalar.copy(out=y_sb[:], in_=y[:])
+            for i in range(2):
+                t = 2 * e + i
+                nc.vector.tensor_tensor(out=res[c][:, t, :], in0=r_tab[t][:].indirect(picks(j0, width)), in1=y_sb[:, i, :], op=ALU.add)
+            nc.sync.dma_start(out=out_rows[:, 2 * e : 2 * e + 2, cols], in_=res[c][:, 2 * e : 2 * e + 2, :])
+
+        def planes(c):
+            j0, width = pieces[c]
+            cols = slice(j0, j0 + width)
+            o_b = ring.tile([P, width, PACK], BF16, name="o_b", align_bytes=64)
+            eng = nc.vector.tensor_copy if c >= len(pieces) - 1 else nc.scalar.copy
+            eng(
+                out=o_b[:].rearrange("p (a i) t -> p a t i", i=4),
+                in_=res[c][:].rearrange("p t (a i) -> p a t i", i=4),
+            )
+            o_w = ring.tile([P, width], U32, name="o_w", align_bytes=64, bufs=len(pieces))
+            nc.vector.quantize_mx(out=o_w[:].bitcast(FP8X4), scales=o_s[:, cols], in_=o_b[:].rearrange("p n t -> p (n t)"))
+            nc.sync.dma_start(out=words_out[:, cols], in_=o_w[:].bitcast(I32))
+
+        for c in range(len(pieces)):
+            pair(c, 0)
+        for c in range(len(pieces)):
+            pair(c, 1)
+            if c > 0:
+                planes(c - 1)
+        planes(len(pieces) - 1)
+        for q in range(4):
+            queue = nc.scalar if q % 2 else nc.sync
+            queue.dma_start(out=out_2[0, 4 * q : 4 * q + 4, :].bitcast(I32), in_=o_s[32 * q : 32 * q + 4, :].bitcast(I32))

@@ -34,14 +34,15 @@ def tile_list_gmlpt_relu_resLP_kernel(
     with ExitStack() as ctx:
         keep = ctx.enter_context(tc.tile_pool(name="keep", bufs=1))
         ring = ctx.enter_context(tc.tile_pool(name="ring", bufs=2))
-        psum = ctx.enter_context(tc.psum_pool(name="psum", bufs=2))
+        psum = ctx.enter_context(tc.psum_pool(name="psum", bufs=4))
 
         offsets = keep.tile([P, J // 16], U16, name="offsets")
         tab_s = keep.tile([P, T], U8, name="tab_s", align_bytes=64)
-        wu_s_raw = keep.tile([P, R], U8, name="wu_s_raw", align_bytes=64)
+        wu_s_raw = keep.tile([P, R], U8, name="wu_s_raw", tag="late_words", align_bytes=64)
         tab_w = keep.tile([P, T], I32, name="tab_w", align_bytes=64)
         wu_w_raw = keep.tile([P, R // 2], I32, name="wu_w_raw", align_bytes=64)
-        wg_raw = [keep.tile([P, PACK, R // 2], F32, name="wg_raw%d" % u) for u in range(2)]
+        wg_all = keep.tile([P, 2, PACK, R // 2], F32, name="wg_all", tag="wg_then_ub")
+        wg_raw = [wg_all[:, u] for u in range(2)]
         wd_raw = keep.tile([P, PACK, N], F32, name="wd_raw")
         r_tab = [keep.tile([P, T], F32, name="r_tab%d" % t) for t in range(PACK)]
 
@@ -56,15 +57,15 @@ def tile_list_gmlpt_relu_resLP_kernel(
             nc.sync.dma_start(out=tab_w[:], in_=tab_words[0].rearrange("p t i -> p (t i)").bitcast(I32))
 
         def load_wg(u):
-            nc.sync.dma_start(out=wg_raw[u][:], in_=wg.rearrange("(p j) r -> p j r", j=PACK)[:, :, u * (R // 2) : (u + 1) * (R // 2)])
+            nc.sync.dma_start(out=wg_raw[u], in_=wg.rearrange("(p j) r -> p j r", j=PACK)[:, :, u * (R // 2) : (u + 1) * (R // 2)])
 
         nc.sync.dma_start(offsets[:], offs)
         load_scale_rows(tab_s, tab_scales)
         nc.sync.dma_start(out=wu_w_raw[:], in_=wu_words[0].bitcast(I32))
-        load_wg(0)
-        load_wg(1)
         load_tab_w()
         load_scale_rows(wu_s_raw, wu_scales)
+        load_wg(0)
+        load_wg(1)
         r_rows = rT.rearrange("(p t) c -> t p c", t=PACK)
         nc.sync.dma_start(out=wd_raw[:], in_=wd.rearrange("(p j) n -> p j n", j=PACK))
         for t in range(PACK):
@@ -81,6 +82,11 @@ def tile_list_gmlpt_relu_resLP_kernel(
         nc.scalar.copy(out=wu_w[:], in_=wu_w_raw[:].bitcast(U16).rearrange("p (m t) -> p t m", t=PACK))
         nc.vector.tensor_copy(out=wu_s[:], in_=wu_s_raw[:].rearrange("p (m t) -> p t m", t=PACK))
 
+        v_w = []
+        for u, tag in enumerate(("early_words", "late_words")):
+            v_w.append(keep.tile([P, J // 2], U32, name="v_w%d" % u, tag=tag, align_bytes=64))
+            nc.vector.tensor_copy(out=v_w[u][:], in_=tab_w[:].bitcast(U32).indirect(picks(u * (J // 2), J // 2)))
+
         def round_and_deal(dst, src, m0, count, eng):
             eng(
                 out=dst[:, :, m0 : m0 + count, :].rearrange("p t m j -> p m t j"),
@@ -88,16 +94,12 @@ def tile_list_gmlpt_relu_resLP_kernel(
             )
 
         wg_b = keep.tile([P, PACK, P, PACK], BF16, name="wg_b", align_bytes=64)
-        round_and_deal(wg_b, wg_raw[0][:], 0, P // 2, nc.scalar.copy)
-        round_and_deal(wg_b, wg_raw[1][:], P // 2, P // 2, nc.scalar.copy)
+        round_and_deal(wg_b, wg_raw[0], 0, P // 2, nc.scalar.copy)
+        round_and_deal(wg_b, wg_raw[1][:, :, 0:P], P // 2, P // 4, nc.scalar.copy)
+        round_and_deal(wg_b, wg_raw[1][:, :, P : 2 * P], 3 * P // 4, P // 4, nc.vector.tensor_copy)
         wg_w = keep.tile([P, R], U32, name="wg_w", align_bytes=64)
         wg_s = keep.tile([P, R], U8, name="wg_s", align_bytes=64)
         nc.vector.quantize_mx(out=wg_w[:].bitcast(FP8X4), scales=wg_s[:], in_=wg_b[:].rearrange("p t m j -> p (t m j)"))
-
-        v_w = keep.tile([P, J], U32, name="v_w", align_bytes=64)
-
-        def gather_words(j0, width):
-            nc.vector.tensor_copy(out=v_w[:, j0 : j0 + width], in_=tab_w[:].bitcast(U32).indirect(picks(j0, width)))
 
         wd_b = keep.tile([P, PACK, P, PACK], BF16, name="wd_b", align_bytes=64)
         wd_w = keep.tile([P, N], U32, name="wd_w", align_bytes=64)
@@ -107,33 +109,32 @@ def tile_list_gmlpt_relu_resLP_kernel(
         h_s = keep.tile([P, J], U8, name="h_s", align_bytes=64)
         h_b = keep.tile([P, J * PACK], BF16, name="h_b", align_bytes=64)
 
+        ub_all = keep.tile([P, J, PACK], F32, name="ub_all", tag="wg_then_ub")
+
         def hidden(j0):
             cols = slice(j0, j0 + STEP)
-            moving = v_w[:, cols].bitcast(FP8X4)
-            ub = psum.tile([P, PACK, STEP], F32, name="ub")
-            ga = psum.tile([P, PACK, STEP], F32, name="ga")
+            u, a = divmod(j0, J // 2)
+            moving = v_w[u][:, a : a + STEP].bitcast(FP8X4)
+            ub = psum.tile([P, PACK, STEP], F32, name="ub", tag="bank0")
+            ga = psum.tile([P, PACK, STEP], F32, name="ga", tag="bank1")
             for t in range(PACK):
                 nc.tensor.matmul_mx(out=ub[:, t, :], lhsT=wu_w[:, t, :].bitcast(FP4X4), lhsT_scale=wu_s[:, t, :], rhs=moving, rhs_scale=v_s[:, cols], start=True, stop=True)
             for t in range(PACK):
                 m = slice(t * P, (t + 1) * P)
                 nc.tensor.matmul_mx(out=ga[:, t, :], lhsT=wg_w[:, m].bitcast(FP8X4), lhsT_scale=wg_s[:, m], rhs=moving, rhs_scale=v_s[:, cols], start=True, stop=True)
-            ub_sb = ring.tile([P, STEP, PACK], F32, name="ub_sb", bufs=4)
-            nc.scalar.copy(out=ub_sb[:], in_=ub[:].rearrange("p t n -> p n t"))
+            ub_sb = ub_all[:, cols, :]
+            nc.scalar.copy(out=ub_sb, in_=ub[:].rearrange("p t n -> p n t"))
             nc.vector.scalar_tensor_tensor(
                 out=h_b[:, j0 * PACK : (j0 + STEP) * PACK].rearrange("p (n t) -> p n t", t=PACK),
-                in0=ga[:].rearrange("p t n -> p n t"), scalar=0.0, in1=ub_sb[:], op0=ALU.max, op1=ALU.mult,
+                in0=ga[:].rearrange("p t n -> p n t"), scalar=0.0, in1=ub_sb, op0=ALU.max, op1=ALU.mult,
             )
 
         def quantize_h(j0):
             cols = slice(j0, j0 + CHUNK)
             nc.vector.quantize_mx(out=h_w[:, cols].bitcast(FP8X4), scales=h_s[:, cols], in_=h_b[:, j0 * PACK : (j0 + CHUNK) * PACK])
 
-        word_pieces = dict(starts(WORD_PIECES))
-        gather_words(0, word_pieces[0])
         for s in range(J // STEP):
             j0 = s * STEP
-            if j0 + STEP in word_pieces:
-                gather_words(j0 + STEP, word_pieces[j0 + STEP])
             hidden(j0)
             if j0 % CHUNK == 0 and j0 > 0:
                 quantize_h(j0 - CHUNK)
@@ -150,10 +151,10 @@ def tile_list_gmlpt_relu_resLP_kernel(
         o_s = keep.tile([P, J], U8, name="o_s", align_bytes=64)
         words_out = out_1[0].rearrange("p j i -> p (j i)").bitcast(I32)
 
-        def pair(c, e):
+        def product(c, e):
             j0, width = pieces[c]
             cols = slice(j0, j0 + width)
-            y = psum.tile([P, 2, width], F32, name="y%d" % e)
+            y = psum.tile([P, 2, width], F32, name="y%d" % e, tag="bank%d" % e)
             for i in range(2):
                 m = slice((2 * e + i) * P, (2 * e + i + 1) * P)
                 nc.tensor.matmul_mx(
@@ -162,6 +163,14 @@ def tile_list_gmlpt_relu_resLP_kernel(
                 )
             y_sb = ring.tile([P, 2, width], F32, name="y_sb%d" % e, bufs=len(pieces))
             nc.scalar.copy(out=y_sb[:], in_=y[:])
+            return y_sb
+
+        y_pairs = {(c, e): product(c, e) for e in range(2) for c in range(len(pieces))}
+
+        def pair(c, e):
+            j0, width = pieces[c]
+            cols = slice(j0, j0 + width)
+            y_sb = y_pairs[c, e]
             for i in range(2):
                 t = 2 * e + i
                 nc.vector.tensor_tensor(out=res[c][:, t, :], in0=r_tab[t][:].indirect(picks(j0, width)), in1=y_sb[:, i, :], op=ALU.add)

@@ -16,15 +16,11 @@ FP4X4 = mybir.dt.float4_e2m1fn_x4
 ALU = mybir.AluOpType
 
 P = 128
-PACK = 4
+SLOTS = 4
+HALF = J // 2
 STEP = 128
-CHUNK = 256
-WORD_PIECES = (256, 256, 512)
-OUT_PIECES = (256, 256, 256, 128, 128)
-
-
-def starts(widths):
-    return [(sum(widths[:i]), w) for i, w in enumerate(widths)]
+H_CHUNK = 256
+PIECES = (256, 256, 256, 128, 128)
 
 
 def tile_list_gmlpt_relu_resLP_kernel(
@@ -33,18 +29,16 @@ def tile_list_gmlpt_relu_resLP_kernel(
     nc = tc.nc
     with ExitStack() as ctx:
         keep = ctx.enter_context(tc.tile_pool(name="keep", bufs=1))
-        ring = ctx.enter_context(tc.tile_pool(name="ring", bufs=2))
         psum = ctx.enter_context(tc.psum_pool(name="psum", bufs=4))
 
         offsets = keep.tile([P, J // 16], U16, name="offsets")
         tab_s = keep.tile([P, T], U8, name="tab_s", align_bytes=64)
-        wu_s_raw = keep.tile([P, R], U8, name="wu_s_raw", tag="late_words", align_bytes=64)
         tab_w = keep.tile([P, T], I32, name="tab_w", align_bytes=64)
+        wu_s_raw = keep.tile([P, R], U8, name="wu_s_raw", tag="wu_s_then_words", align_bytes=64)
         wu_w_raw = keep.tile([P, R // 2], I32, name="wu_w_raw", align_bytes=64)
-        wg_all = keep.tile([P, 2, PACK, R // 2], F32, name="wg_all", tag="wg_then_ub")
-        wg_raw = [wg_all[:, u] for u in range(2)]
-        wd_raw = keep.tile([P, PACK, N], F32, name="wd_raw")
-        r_tab = [keep.tile([P, T], F32, name="r_tab%d" % t) for t in range(PACK)]
+        wg_raw = keep.tile([P, 2, SLOTS, R // 2], F32, name="wg_raw", tag="wg_then_ub")
+        wd_raw = keep.tile([P, SLOTS, N], F32, name="wd_raw")
+        r_tab = [keep.tile([P, T], F32, name="r_tab%d" % t) for t in range(SLOTS)]
 
         nc.vector.memset(tab_s[:].bitcast(I32), 0)
         nc.vector.memset(wu_s_raw[:].bitcast(I32), 0)
@@ -53,149 +47,154 @@ def tile_list_gmlpt_relu_resLP_kernel(
             for q in range(4):
                 nc.sync.dma_start(out=plane[32 * q : 32 * q + 4, :].bitcast(I32), in_=rows[0, 4 * q : 4 * q + 4, :].bitcast(I32))
 
-        def load_tab_w():
-            nc.sync.dma_start(out=tab_w[:], in_=tab_words[0].rearrange("p t i -> p (t i)").bitcast(I32))
-
-        def load_wg(u):
-            nc.sync.dma_start(out=wg_raw[u], in_=wg.rearrange("(p j) r -> p j r", j=PACK)[:, :, u * (R // 2) : (u + 1) * (R // 2)])
-
         nc.sync.dma_start(offsets[:], offs)
         load_scale_rows(tab_s, tab_scales)
         nc.sync.dma_start(out=wu_w_raw[:], in_=wu_words[0].bitcast(I32))
-        load_tab_w()
+        nc.sync.dma_start(out=tab_w[:], in_=tab_words[0].rearrange("p t i -> p (t i)").bitcast(I32))
         load_scale_rows(wu_s_raw, wu_scales)
-        load_wg(0)
-        load_wg(1)
-        r_rows = rT.rearrange("(p t) c -> t p c", t=PACK)
-        nc.sync.dma_start(out=wd_raw[:], in_=wd.rearrange("(p j) n -> p j n", j=PACK))
-        for t in range(PACK):
-            nc.sync.dma_start(out=r_tab[t][:], in_=r_rows[t])
+        for u in range(2):
+            nc.sync.dma_start(out=wg_raw[:, u], in_=wg.rearrange("(p s) r -> p s r", s=SLOTS)[:, :, u * (R // 2) : (u + 1) * (R // 2)])
+        nc.sync.dma_start(out=wd_raw[:], in_=wd.rearrange("(p s) n -> p s n", s=SLOTS))
+        for t in range(SLOTS):
+            nc.sync.dma_start(out=r_tab[t][:], in_=rT.rearrange("(p t) c -> t p c", t=SLOTS)[t])
 
-        def picks(j0, width):
+        def entries(j0, width):
             return offsets[:, j0 // 16 : (j0 + width) // 16]
 
         v_s = keep.tile([P, J], U8, name="v_s", align_bytes=64)
         nc.vector.tensor_copy(out=v_s[:], in_=tab_s[:].indirect(offsets[:]))
 
-        wu_w = keep.tile([P, PACK, P], U16, name="wu_w", align_bytes=64)
-        wu_s = keep.tile([P, PACK, P], U8, name="wu_s", align_bytes=64)
-        nc.scalar.copy(out=wu_w[:], in_=wu_w_raw[:].bitcast(U16).rearrange("p (m t) -> p t m", t=PACK))
-        nc.vector.tensor_copy(out=wu_s[:], in_=wu_s_raw[:].rearrange("p (m t) -> p t m", t=PACK))
+        wu_w = keep.tile([P, SLOTS, P], U16, name="wu_w", align_bytes=64)
+        wu_s = keep.tile([P, SLOTS, P], U8, name="wu_s", align_bytes=64)
+        nc.scalar.copy(out=wu_w[:], in_=wu_w_raw[:].bitcast(U16).rearrange("p (m t) -> p t m", t=SLOTS))
+        nc.vector.tensor_copy(out=wu_s[:], in_=wu_s_raw[:].rearrange("p (m t) -> p t m", t=SLOTS))
 
         v_w = []
-        for u, tag in enumerate(("early_words", "late_words")):
-            v_w.append(keep.tile([P, J // 2], U32, name="v_w%d" % u, tag=tag, align_bytes=64))
-            nc.vector.tensor_copy(out=v_w[u][:], in_=tab_w[:].bitcast(U32).indirect(picks(u * (J // 2), J // 2)))
+        for u, tag in enumerate(("words", "wu_s_then_words")):
+            v_w.append(keep.tile([P, HALF], U32, name="v_w%d" % u, tag=tag, align_bytes=64))
+            nc.vector.tensor_copy(out=v_w[u][:], in_=tab_w[:].bitcast(U32).indirect(entries(u * HALF, HALF)))
 
-        def round_and_deal(dst, src, m0, count, eng):
-            eng(
-                out=dst[:, :, m0 : m0 + count, :].rearrange("p t m j -> p m t j"),
-                in_=src.rearrange("p j (m t) -> p m t j", t=PACK),
+        def round_and_deal(copy, dst, src, col0):
+            m0, count = col0 // SLOTS, src.shape[2] // SLOTS
+            copy(
+                out=dst[:, :, m0 : m0 + count, :].rearrange("p t m s -> p m t s"),
+                in_=src.rearrange("p s (m t) -> p m t s", t=SLOTS),
             )
 
-        wg_b = keep.tile([P, PACK, P, PACK], BF16, name="wg_b", align_bytes=64)
-        round_and_deal(wg_b, wg_raw[0], 0, P // 2, nc.scalar.copy)
-        round_and_deal(wg_b, wg_raw[1][:, :, 0:P], P // 2, P // 4, nc.scalar.copy)
-        round_and_deal(wg_b, wg_raw[1][:, :, P : 2 * P], 3 * P // 4, P // 4, nc.vector.tensor_copy)
-        wg_w = keep.tile([P, R], U32, name="wg_w", align_bytes=64)
-        wg_s = keep.tile([P, R], U8, name="wg_s", align_bytes=64)
-        nc.vector.quantize_mx(out=wg_w[:].bitcast(FP8X4), scales=wg_s[:], in_=wg_b[:].rearrange("p t m j -> p (t m j)"))
+        def quantize_weight(name, rounded):
+            words = keep.tile([P, SLOTS * P], U32, name=name + "_w", align_bytes=64)
+            scales = keep.tile([P, SLOTS * P], U8, name=name + "_s", align_bytes=64)
+            nc.vector.quantize_mx(out=words[:].bitcast(FP8X4), scales=scales[:], in_=rounded[:].rearrange("p t m s -> p (t m s)"))
+            return words, scales
 
-        wd_b = keep.tile([P, PACK, P, PACK], BF16, name="wd_b", align_bytes=64)
-        wd_w = keep.tile([P, N], U32, name="wd_w", align_bytes=64)
-        wd_s = keep.tile([P, N], U8, name="wd_s", align_bytes=64)
+        wg_b = keep.tile([P, SLOTS, P, SLOTS], BF16, name="wg_b", align_bytes=64)
+        round_and_deal(nc.scalar.copy, wg_b, wg_raw[:, 0], 0)
+        round_and_deal(nc.scalar.copy, wg_b, wg_raw[:, 1, :, 0 : R // 4], R // 2)
+        round_and_deal(nc.vector.tensor_copy, wg_b, wg_raw[:, 1, :, R // 4 : R // 2], 3 * R // 4)
+        wg_w, wg_s = quantize_weight("wg", wg_b)
 
+        ub_sb = keep.tile([P, J, SLOTS], F32, name="ub_sb", tag="wg_then_ub")
+        h_b = keep.tile([P, J * SLOTS], BF16, name="h_b", align_bytes=64)
         h_w = keep.tile([P, J], U32, name="h_w", align_bytes=64)
         h_s = keep.tile([P, J], U8, name="h_s", align_bytes=64)
-        h_b = keep.tile([P, J * PACK], BF16, name="h_b", align_bytes=64)
-
-        ub_all = keep.tile([P, J, PACK], F32, name="ub_all", tag="wg_then_ub")
 
         def hidden(j0):
             cols = slice(j0, j0 + STEP)
-            u, a = divmod(j0, J // 2)
+            u, a = divmod(j0, HALF)
             moving = v_w[u][:, a : a + STEP].bitcast(FP8X4)
-            ub = psum.tile([P, PACK, STEP], F32, name="ub", tag="bank0")
-            ga = psum.tile([P, PACK, STEP], F32, name="ga", tag="bank1")
-            for t in range(PACK):
-                nc.tensor.matmul_mx(out=ub[:, t, :], lhsT=wu_w[:, t, :].bitcast(FP4X4), lhsT_scale=wu_s[:, t, :], rhs=moving, rhs_scale=v_s[:, cols], start=True, stop=True)
-            for t in range(PACK):
-                m = slice(t * P, (t + 1) * P)
-                nc.tensor.matmul_mx(out=ga[:, t, :], lhsT=wg_w[:, m].bitcast(FP8X4), lhsT_scale=wg_s[:, m], rhs=moving, rhs_scale=v_s[:, cols], start=True, stop=True)
-            ub_sb = ub_all[:, cols, :]
-            nc.scalar.copy(out=ub_sb, in_=ub[:].rearrange("p t n -> p n t"))
+            ub = psum.tile([P, SLOTS, STEP], F32, name="ub", tag="bank0")
+            ga = psum.tile([P, SLOTS, STEP], F32, name="ga", tag="bank1")
+            for t in range(SLOTS):
+                nc.tensor.matmul_mx(
+                    out=ub[:, t, :], lhsT=wu_w[:, t, :].bitcast(FP4X4), lhsT_scale=wu_s[:, t, :],
+                    rhs=moving, rhs_scale=v_s[:, cols], start=True, stop=True,
+                )
+            for t in range(SLOTS):
+                places = slice(t * P, (t + 1) * P)
+                nc.tensor.matmul_mx(
+                    out=ga[:, t, :], lhsT=wg_w[:, places].bitcast(FP8X4), lhsT_scale=wg_s[:, places],
+                    rhs=moving, rhs_scale=v_s[:, cols], start=True, stop=True,
+                )
+            nc.scalar.copy(out=ub_sb[:, cols, :], in_=ub[:].rearrange("p t n -> p n t"))
             nc.vector.scalar_tensor_tensor(
-                out=h_b[:, j0 * PACK : (j0 + STEP) * PACK].rearrange("p (n t) -> p n t", t=PACK),
-                in0=ga[:].rearrange("p t n -> p n t"), scalar=0.0, in1=ub_sb, op0=ALU.max, op1=ALU.mult,
+                out=h_b[:, j0 * SLOTS : (j0 + STEP) * SLOTS].rearrange("p (n t) -> p n t", t=SLOTS),
+                in0=ga[:].rearrange("p t n -> p n t"), scalar=0.0, in1=ub_sb[:, cols, :], op0=ALU.max, op1=ALU.mult,
             )
 
         def quantize_h(j0):
-            cols = slice(j0, j0 + CHUNK)
-            nc.vector.quantize_mx(out=h_w[:, cols].bitcast(FP8X4), scales=h_s[:, cols], in_=h_b[:, j0 * PACK : (j0 + CHUNK) * PACK])
+            cols = slice(j0, j0 + H_CHUNK)
+            nc.vector.quantize_mx(out=h_w[:, cols].bitcast(FP8X4), scales=h_s[:, cols], in_=h_b[:, j0 * SLOTS : (j0 + H_CHUNK) * SLOTS])
 
-        for s in range(J // STEP):
-            j0 = s * STEP
+        wd_b = keep.tile([P, SLOTS, P, SLOTS], BF16, name="wd_b", align_bytes=64)
+        quarter = N // 4
+        for step in range(J // STEP):
+            j0 = step * STEP
             hidden(j0)
-            if j0 % CHUNK == 0 and j0 > 0:
-                quantize_h(j0 - CHUNK)
-            if 1 <= s < 1 + 4:
-                i = s - 1
-                round_and_deal(wd_b, wd_raw[:, :, i * P : (i + 1) * P], i * (P // 4), P // 4, nc.scalar.copy)
-            if s == 1 + 4:
-                nc.vector.quantize_mx(out=wd_w[:].bitcast(FP8X4), scales=wd_s[:], in_=wd_b[:].rearrange("p t m j -> p (t m j)"))
-        quantize_h(J - CHUNK)
+            if j0 % H_CHUNK == 0 and j0 > 0:
+                quantize_h(j0 - H_CHUNK)
+            if 1 <= step <= 4:
+                n0 = (step - 1) * quarter
+                round_and_deal(nc.scalar.copy, wd_b, wd_raw[:, :, n0 : n0 + quarter], n0)
+            if step == 5:
+                wd_w, wd_s = quantize_weight("wd", wd_b)
+        quantize_h(J - H_CHUNK)
 
-        pieces = starts(OUT_PIECES)
-        res = [keep.tile([P, PACK, w], F32, name="res%d" % j0) for j0, w in pieces]
-        out_rows = out_0.rearrange("(p t) j -> p t j", t=PACK)
+        res = [keep.tile([P, SLOTS, HALF], F32, name="res%d" % u) for u in range(2)]
+        out_rows = out_0.rearrange("(p t) j -> p t j", t=SLOTS)
+        out_words = out_1[0].rearrange("p j i -> p (j i)").bitcast(I32)
         o_s = keep.tile([P, J], U8, name="o_s", align_bytes=64)
-        words_out = out_1[0].rearrange("p j i -> p (j i)").bitcast(I32)
 
-        def product(c, e):
-            j0, width = pieces[c]
-            cols = slice(j0, j0 + width)
-            y = psum.tile([P, 2, width], F32, name="y%d" % e, tag="bank%d" % e)
-            for i in range(2):
-                m = slice((2 * e + i) * P, (2 * e + i + 1) * P)
-                nc.tensor.matmul_mx(
-                    out=y[:, i, :], lhsT=wd_w[:, m].bitcast(FP8X4), lhsT_scale=wd_s[:, m],
-                    rhs=h_w[:, cols].bitcast(FP8X4), rhs_scale=h_s[:, cols], start=True, stop=True,
-                )
-            y_sb = ring.tile([P, 2, width], F32, name="y_sb%d" % e, bufs=len(pieces))
-            nc.scalar.copy(out=y_sb[:], in_=y[:])
-            return y_sb
-
-        y_pairs = {(c, e): product(c, e) for e in range(2) for c in range(len(pieces))}
-
-        def pair(c, e):
-            j0, width = pieces[c]
-            cols = slice(j0, j0 + width)
-            y_sb = y_pairs[c, e]
-            for i in range(2):
-                t = 2 * e + i
-                nc.vector.tensor_tensor(out=res[c][:, t, :], in0=r_tab[t][:].indirect(picks(j0, width)), in1=y_sb[:, i, :], op=ALU.add)
-            nc.sync.dma_start(out=out_rows[:, 2 * e : 2 * e + 2, cols], in_=res[c][:, 2 * e : 2 * e + 2, :])
-
-        def planes(c):
-            j0, width = pieces[c]
-            cols = slice(j0, j0 + width)
-            o_b = ring.tile([P, width, PACK], BF16, name="o_b", align_bytes=64)
-            eng = nc.vector.tensor_copy if c >= len(pieces) - 1 else nc.scalar.copy
-            eng(
-                out=o_b[:].rearrange("p (a i) t -> p a t i", i=4),
-                in_=res[c][:].rearrange("p t (a i) -> p a t i", i=4),
+        def product(u, t, y_sb):
+            cols = slice(u * HALF, (u + 1) * HALF)
+            places = slice(t * P, (t + 1) * P)
+            y = psum.tile([P, HALF], F32, name="y", tag="bank%d" % (t % 2))
+            nc.tensor.matmul_mx(
+                out=y[:], lhsT=wd_w[:, places].bitcast(FP8X4), lhsT_scale=wd_s[:, places],
+                rhs=h_w[:, cols].bitcast(FP8X4), rhs_scale=h_s[:, cols], start=True, stop=True,
             )
-            o_w = ring.tile([P, width], U32, name="o_w", align_bytes=64, bufs=len(pieces))
-            nc.vector.quantize_mx(out=o_w[:].bitcast(FP8X4), scales=o_s[:, cols], in_=o_b[:].rearrange("p n t -> p (n t)"))
-            nc.sync.dma_start(out=words_out[:, cols], in_=o_w[:].bitcast(I32))
+            nc.scalar.copy(out=y_sb, in_=y[:])
 
-        for c in range(len(pieces)):
-            pair(c, 0)
-        for c in range(len(pieces)):
-            pair(c, 1)
-            if c > 0:
-                planes(c - 1)
-        planes(len(pieces) - 1)
+        def add_residual(u, t, y_sb, a, width):
+            j0 = u * HALF + a
+            nc.vector.tensor_tensor(
+                out=res[u][:, t, a : a + width], in0=r_tab[t][:].indirect(entries(j0, width)), in1=y_sb[:, a : a + width], op=ALU.add
+            )
+            nc.sync.dma_start(out=out_rows[:, t, j0 : j0 + width], in_=res[u][:, t, a : a + width])
+
+        def planes(copy, j0, width):
+            cols = slice(j0, j0 + width)
+            u, a = divmod(j0, HALF)
+            o_b = keep.tile([P, width, SLOTS], BF16, name="o_b%d" % j0, align_bytes=64)
+            o_w = keep.tile([P, width], U32, name="o_w%d" % j0, align_bytes=64)
+            copy(
+                out=o_b[:].rearrange("p (c i) t -> p c t i", i=4),
+                in_=res[u][:, :, a : a + width].rearrange("p t (c i) -> p c t i", i=4),
+            )
+            nc.vector.quantize_mx(out=o_w[:].bitcast(FP8X4), scales=o_s[:, cols], in_=o_b[:].rearrange("p n t -> p (n t)"))
+            nc.sync.dma_start(out=out_words[:, cols], in_=o_w[:].bitcast(I32))
+
+        early = [(0, 0), (0, 1), (1, 0), (0, 2), (0, 3), (1, 3)]
+        late = [(1, 1), (1, 2)]
+        y_early = {}
+        for u, t in early:
+            tag = "y03_then_late" if (u, t) == (0, 3) else "y%d%d" % (u, t)
+            y_early[u, t] = keep.tile([P, HALF], F32, name="y_sb%d%d" % (u, t), tag=tag)
+            product(u, t, y_early[u, t][:])
+        for u, t in early:
+            add_residual(u, t, y_early[u, t][:], 0, HALF)
+        y_late = keep.tile([P, len(late), HALF], F32, name="y_late", tag="y03_then_late")
+        for i, (u, t) in enumerate(late):
+            product(u, t, y_late[:, i, :])
+        add_residual(*late[0], y_late[:, 0, :], 0, HALF)
+
+        pieces = [(sum(PIECES[:i]), width) for i, width in enumerate(PIECES)]
+        for j0, width in pieces:
+            if j0 >= HALF:
+                add_residual(*late[1], y_late[:, 1, :], j0 - HALF, width)
+        for j0, width in pieces[:-1]:
+            planes(nc.scalar.copy, j0, width)
+        planes(nc.vector.tensor_copy, *pieces[-1])
+
         for q in range(4):
             queue = nc.scalar if q % 2 else nc.sync
             queue.dma_start(out=out_2[0, 4 * q : 4 * q + 4, :].bitcast(I32), in_=o_s[32 * q : 32 * q + 4, :].bitcast(I32))

from contextlib import ExitStack

import concourse.mybir as mybir

K, R, N, T, J = 512, 512, 512, 2048, 1024
FLOPS = 2 * J * (K * R + K * R + R * N)

F32 = mybir.dt.float32
BF16 = mybir.dt.bfloat16
I32 = mybir.dt.int32
U32 = mybir.dt.uint32
U16 = mybir.dt.uint16
U8 = mybir.dt.uint8
FP8X4 = mybir.dt.float8_e4m3fn_x4
FP4X4 = mybir.dt.float4_e2m1fn_x4
ALU = mybir.AluOpType

P = 128
SLOTS = 4
HALF = J // 2
STEP = 128
H_CHUNK = 256
PIECES = (256, 256, 256, 128, 128)


def tile_list_gmlpt_relu_resLP_kernel(
    tc, tab_words, tab_scales, wg, wu_words, wu_scales, wd, rT, offs, out_0, out_1, out_2
):
    nc = tc.nc
    with ExitStack() as ctx:
        keep = ctx.enter_context(tc.tile_pool(name="keep", bufs=1))
        psum = ctx.enter_context(tc.psum_pool(name="psum", bufs=4))

        offsets = keep.tile([P, J // 16], U16, name="offsets")
        tab_s = keep.tile([P, T], U8, name="tab_s", align_bytes=64)
        tab_w = keep.tile([P, T], I32, name="tab_w", align_bytes=64)
        wu_s_raw = keep.tile([P, R], U8, name="wu_s_raw", tag="wu_s_then_words", align_bytes=64)
        wu_w_raw = keep.tile([P, R // 2], I32, name="wu_w_raw", align_bytes=64)
        wg_raw = keep.tile([P, 2, SLOTS, R // 2], F32, name="wg_raw", tag="wg_then_ub")
        wd_raw = keep.tile([P, SLOTS, N], F32, name="wd_raw")
        r_tab = [keep.tile([P, T], F32, name="r_tab%d" % t) for t in range(SLOTS)]

        nc.vector.memset(tab_s[:].bitcast(I32), 0)
        nc.vector.memset(wu_s_raw[:].bitcast(I32), 0)

        def load_scale_rows(plane, rows):
            for q in range(4):
                nc.sync.dma_start(out=plane[32 * q : 32 * q + 4, :].bitcast(I32), in_=rows[0, 4 * q : 4 * q + 4, :].bitcast(I32))

        nc.sync.dma_start(offsets[:], offs)
        load_scale_rows(tab_s, tab_scales)
        nc.sync.dma_start(out=wu_w_raw[:], in_=wu_words[0].bitcast(I32))
        nc.sync.dma_start(out=tab_w[:], in_=tab_words[0].rearrange("p t i -> p (t i)").bitcast(I32))
        load_scale_rows(wu_s_raw, wu_scales)
        for u in range(2):
            nc.sync.dma_start(out=wg_raw[:, u], in_=wg.rearrange("(p s) r -> p s r", s=SLOTS)[:, :, u * (R // 2) : (u + 1) * (R // 2)])
        nc.sync.dma_start(out=wd_raw[:], in_=wd.rearrange("(p s) n -> p s n", s=SLOTS))
        for t in range(SLOTS):
            nc.sync.dma_start(out=r_tab[t][:], in_=rT.rearrange("(p t) c -> t p c", t=SLOTS)[t])

        def entries(j0, width):
            return offsets[:, j0 // 16 : (j0 + width) // 16]

        v_s = keep.tile([P, J], U8, name="v_s", align_bytes=64)
        nc.vector.tensor_copy(out=v_s[:], in_=tab_s[:].indirect(offsets[:]))

        wu_w = keep.tile([P, SLOTS, P], U16, name="wu_w", align_bytes=64)
        wu_s = keep.tile([P, SLOTS, P], U8, name="wu_s", align_bytes=64)
        nc.scalar.copy(out=wu_w[:], in_=wu_w_raw[:].bitcast(U16).rearrange("p (m t) -> p t m", t=SLOTS))
        nc.vector.tensor_copy(out=wu_s[:], in_=wu_s_raw[:].rearrange("p (m t) -> p t m", t=SLOTS))

        v_w = []
        for u, tag in enumerate(("words", "wu_s_then_words")):
            v_w.append(keep.tile([P, HALF], U32, name="v_w%d" % u, tag=tag, align_bytes=64))
            nc.vector.tensor_copy(out=v_w[u][:], in_=tab_w[:].bitcast(U32).indirect(entries(u * HALF, HALF)))

        def round_and_deal(copy, dst, src, col0):
            m0, count = col0 // SLOTS, src.shape[2] // SLOTS
            copy(
                out=dst[:, :, m0 : m0 + count, :].rearrange("p t m s -> p m t s"),
                in_=src.rearrange("p s (m t) -> p m t s", t=SLOTS),
            )

        def quantize_weight(name, rounded):
            words = keep.tile([P, SLOTS * P], U32, name=name + "_w", align_bytes=64)
            scales = keep.tile([P, SLOTS * P], U8, name=name + "_s", align_bytes=64)
            nc.vector.quantize_mx(out=words[:].bitcast(FP8X4), scales=scales[:], in_=rounded[:].rearrange("p t m s -> p (t m s)"))
            return words, scales

        wg_b = keep.tile([P, SLOTS, P, SLOTS], BF16, name="wg_b", align_bytes=64)
        round_and_deal(nc.scalar.copy, wg_b, wg_raw[:, 0], 0)
        round_and_deal(nc.scalar.copy, wg_b, wg_raw[:, 1, :, 0 : R // 4], R // 2)
        round_and_deal(nc.vector.tensor_copy, wg_b, wg_raw[:, 1, :, R // 4 : R // 2], 3 * R // 4)
        wg_w, wg_s = quantize_weight("wg", wg_b)

        ub_sb = keep.tile([P, J, SLOTS], F32, name="ub_sb", tag="wg_then_ub")
        h_b = keep.tile([P, J * SLOTS], BF16, name="h_b", align_bytes=64)
        h_w = keep.tile([P, J], U32, name="h_w", align_bytes=64)
        h_s = keep.tile([P, J], U8, name="h_s", align_bytes=64)

        def hidden(j0):
            cols = slice(j0, j0 + STEP)
            u, a = divmod(j0, HALF)
            moving = v_w[u][:, a : a + STEP].bitcast(FP8X4)
            ub = psum.tile([P, SLOTS, STEP], F32, name="ub", tag="bank0")
            ga = psum.tile([P, SLOTS, STEP], F32, name="ga", tag="bank1")
            for t in range(SLOTS):
                nc.tensor.matmul_mx(
                    out=ub[:, t, :], lhsT=wu_w[:, t, :].bitcast(FP4X4), lhsT_scale=wu_s[:, t, :],
                    rhs=moving, rhs_scale=v_s[:, cols], start=True, stop=True,
                )
            for t in range(SLOTS):
                places = slice(t * P, (t + 1) * P)
                nc.tensor.matmul_mx(
                    out=ga[:, t, :], lhsT=wg_w[:, places].bitcast(FP8X4), lhsT_scale=wg_s[:, places],
                    rhs=moving, rhs_scale=v_s[:, cols], start=True, stop=True,
                )
            nc.scalar.copy(out=ub_sb[:, cols, :], in_=ub[:].rearrange("p t n -> p n t"))
            nc.vector.scalar_tensor_tensor(
                out=h_b[:, j0 * SLOTS : (j0 + STEP) * SLOTS].rearrange("p (n t) -> p n t", t=SLOTS),
                in0=ga[:].rearrange("p t n -> p n t"), scalar=0.0, in1=ub_sb[:, cols, :], op0=ALU.max, op1=ALU.mult,
            )

        def quantize_h(j0):
            cols = slice(j0, j0 + H_CHUNK)
            nc.vector.quantize_mx(out=h_w[:, cols].bitcast(FP8X4), scales=h_s[:, cols], in_=h_b[:, j0 * SLOTS : (j0 + H_CHUNK) * SLOTS])

        wd_b = keep.tile([P, SLOTS, P, SLOTS], BF16, name="wd_b", align_bytes=64)
        quarter = N // 4
        for step in range(J // STEP):
            j0 = step * STEP
            hidden(j0)
            if j0 % H_CHUNK == 0 and j0 > 0:
                quantize_h(j0 - H_CHUNK)
            if 1 <= step <= 4:
                n0 = (step - 1) * quarter
                round_and_deal(nc.scalar.copy, wd_b, wd_raw[:, :, n0 : n0 + quarter], n0)
            if step == 5:
                wd_w, wd_s = quantize_weight("wd", wd_b)
        quantize_h(J - H_CHUNK)

        res = [keep.tile([P, SLOTS, HALF], F32, name="res%d" % u) for u in range(2)]
        out_rows = out_0.rearrange("(p t) j -> p t j", t=SLOTS)
        out_words = out_1[0].rearrange("p j i -> p (j i)").bitcast(I32)
        o_s = keep.tile([P, J], U8, name="o_s", align_bytes=64)

        def product(u, t, y_sb):
            cols = slice(u * HALF, (u + 1) * HALF)
            places = slice(t * P, (t + 1) * P)
            y = psum.tile([P, HALF], F32, name="y", tag="bank%d" % (t % 2))
            nc.tensor.matmul_mx(
                out=y[:], lhsT=wd_w[:, places].bitcast(FP8X4), lhsT_scale=wd_s[:, places],
                rhs=h_w[:, cols].bitcast(FP8X4), rhs_scale=h_s[:, cols], start=True, stop=True,
            )
            nc.scalar.copy(out=y_sb, in_=y[:])

        def add_residual(u, t, y_sb, a, width):
            j0 = u * HALF + a
            nc.vector.tensor_tensor(
                out=res[u][:, t, a : a + width], in0=r_tab[t][:].indirect(entries(j0, width)), in1=y_sb[:, a : a + width], op=ALU.add
            )
            nc.sync.dma_start(out=out_rows[:, t, j0 : j0 + width], in_=res[u][:, t, a : a + width])

        def planes(copy, j0, width):
            cols = slice(j0, j0 + width)
            u, a = divmod(j0, HALF)
            o_b = keep.tile([P, width, SLOTS], BF16, name="o_b%d" % j0, align_bytes=64)
            o_w = keep.tile([P, width], U32, name="o_w%d" % j0, align_bytes=64)
            copy(
                out=o_b[:].rearrange("p (c i) t -> p c t i", i=4),
                in_=res[u][:, :, a : a + width].rearrange("p t (c i) -> p c t i", i=4),
            )
            nc.vector.quantize_mx(out=o_w[:].bitcast(FP8X4), scales=o_s[:, cols], in_=o_b[:].rearrange("p n t -> p (n t)"))
            nc.sync.dma_start(out=out_words[:, cols], in_=o_w[:].bitcast(I32))

        early = [(0, 0), (0, 1), (1, 0), (0, 2), (0, 3), (1, 3)]
        late = [(1, 1), (1, 2)]
        y_early = {}
        for u, t in early:
            tag = "y03_then_late" if (u, t) == (0, 3) else "y%d%d" % (u, t)
            y_early[u, t] = keep.tile([P, HALF], F32, name="y_sb%d%d" % (u, t), tag=tag)
            product(u, t, y_early[u, t][:])
        for u, t in early:
            add_residual(u, t, y_early[u, t][:], 0, HALF)
        y_late = keep.tile([P, len(late), HALF], F32, name="y_late", tag="y03_then_late")
        for i, (u, t) in enumerate(late):
            product(u, t, y_late[:, i, :])
        add_residual(*late[0], y_late[:, 0, :], 0, HALF)

        pieces = [(sum(PIECES[:i]), width) for i, width in enumerate(PIECES)]
        for j0, width in pieces:
            if j0 >= HALF:
                add_residual(*late[1], y_late[:, 1, :], j0 - HALF, width)
        for j0, width in pieces[:-1]:
            planes(nc.scalar.copy, j0, width)
        planes(nc.vector.tensor_copy, *pieces[-1])

        for q in range(4):
            queue = nc.scalar if q % 2 else nc.sync
            queue.dma_start(out=out_2[0, 4 * q : 4 * q + 4, :].bitcast(I32), in_=o_s[32 * q : 32 * q + 4, :].bitcast(I32))
